import numpy as np
import ml_dtypes

BF16 = ml_dtypes.bfloat16


def bf(x):
    return np.asarray(x, np.float32).astype(BF16)


def f32(x):
    return np.asarray(x, np.float32)


def f64(x):
    return np.asarray(x).astype(np.float64)


def striped(idx):
    return np.tile(idx.reshape(-1, 16).T, (8, 1))


S, K, M, N = 1024, 256, 128, 1536


def setup_inputs():
    return {"table": bf(np.random.standard_normal((K, S))), "w": bf(np.random.standard_normal((K, M)) / np.sqrt(K)), "b": f32(0.5 * np.random.standard_normal((M, 1))), "offs": striped(np.random.permutation(np.tile(np.arange(S), 2))[:N])}


def reference(table, w, b, offs):
    idx = offs[:16].T.reshape(-1)
    x = f64(table)[:, idx]
    y = f64(w).T @ x
    return y + f64(b)

@@ -1,0 +1,47 @@
+import concourse.mybir as mybir
+
+BF16, F32, U16 = mybir.dt.bfloat16, mybir.dt.float32, mybir.dt.uint16
+
+P = 128
+K, S, M, N = 256, 1024, 128, 1536
+K_BLOCKS = K // P
+PIECE = 512
+PIECES = N // PIECE
+PIECE_COLS = PIECE // 16
+
+FLOPS = 2 * K * M * N
+
+
+def tile_gather_matmul_kernel(tc, table, w, b, offs, out):
+    nc = tc.nc
+    with (
+        tc.tile_pool(name="held", bufs=1) as held,
+        tc.tile_pool(name="staging", bufs=PIECES) as staging,
+        tc.psum_pool(name="psum", bufs=PIECES) as psum,
+    ):
+        offsets = held.tile([P, N // 16], U16, name="offsets")
+        nc.sync.dma_start(offsets[:], offs)
+
+        table_blocks = [held.tile([P, S], BF16, name=f"table{kb}") for kb in range(K_BLOCKS)]
+        w_blocks = [held.tile([P, M], BF16, name=f"w{kb}") for kb in range(K_BLOCKS)]
+        for kb in range(K_BLOCKS):
+            rows = slice(kb * P, (kb + 1) * P)
+            nc.sync.dma_start(w_blocks[kb][:], w[rows, :])
+            nc.sync.dma_start(table_blocks[kb][:], table[rows, :])
+        bias = held.tile([P, 1], F32, name="bias")
+        nc.sync.dma_start(bias[:], b)
+
+        for piece in range(PIECES):
+            piece_offsets = offsets[:, piece * PIECE_COLS : (piece + 1) * PIECE_COLS]
+            bank = psum.tile([P, PIECE], F32, name="bank")
+            for kb in range(K_BLOCKS):
+                nc.tensor.matmul(
+                    bank[:],
+                    w_blocks[kb][:],
+                    table_blocks[kb][:].indirect(piece_offsets),
+                    start=(kb == 0),
+                    stop=(kb == K_BLOCKS - 1),
+                )
+            staged = staging.tile([P, PIECE], F32, name="staged")
+            nc.vector.tensor_scalar(staged[:], bank[:], bias[:, 0:1], None, mybir.AluOpType.add)
+            nc.sync.dma_start(out[:, piece * PIECE : (piece + 1) * PIECE], staged[:])

@@ -5,9 +5,10 @@ BF16, F32, U16 = mybir.dt.bfloat16, mybir.dt.float32, mybir.dt.uint16
 P = 128
 K, S, M, N = 256, 1024, 128, 1536
 K_BLOCKS = K // P
-PIECE = 512
+PIECE = 256
 PIECES = N // PIECE
 PIECE_COLS = PIECE // 16
+WARM_UP = 16
 
 FLOPS = 2 * K * M * N
 
@@ -18,18 +19,26 @@ def tile_gather_matmul_kernel(tc, table, w, b, offs, out):
         tc.tile_pool(name="held", bufs=1) as held,
         tc.tile_pool(name="staging", bufs=PIECES) as staging,
         tc.psum_pool(name="psum", bufs=PIECES) as psum,
+        tc.psum_pool(name="idle", bufs=1) as idle,
     ):
         offsets = held.tile([P, N // 16], U16, name="offsets")
         nc.sync.dma_start(offsets[:], offs)
 
+        weights = held.tile([P, K_BLOCKS, M], BF16, name="weights")
+        nc.scalar.dma_start(weights[:], w.rearrange("(kb p) m -> p kb m", p=P))
+
         table_blocks = [held.tile([P, S], BF16, name=f"table{kb}") for kb in range(K_BLOCKS)]
-        w_blocks = [held.tile([P, M], BF16, name=f"w{kb}") for kb in range(K_BLOCKS)]
-        for kb in range(K_BLOCKS):
-            rows = slice(kb * P, (kb + 1) * P)
-            nc.sync.dma_start(w_blocks[kb][:], w[rows, :])
-            nc.sync.dma_start(table_blocks[kb][:], table[rows, :])
+        nc.sync.dma_start(table_blocks[0][:], table[0:P, :])
+        nc.scalar.dma_start(table_blocks[1][:], table[P : 2 * P, :])
+
         bias = held.tile([P, 1], F32, name="bias")
         nc.sync.dma_start(bias[:], b)
+
+        zeros = held.tile([P, 128], BF16, name="zeros")
+        nc.vector.memset(zeros[:], 0.0)
+        unread = idle.tile([P, 128], F32, name="unread")
+        for i in range(WARM_UP):
+            nc.tensor.matmul(unread[:], zeros[:, :M], zeros[:], start=True, stop=True)
 
         for piece in range(PIECES):
             piece_offsets = offsets[:, piece * PIECE_COLS : (piece + 1) * PIECE_COLS]
@@ -37,11 +46,18 @@ def tile_gather_matmul_kernel(tc, table, w, b, offs, out):
             for kb in range(K_BLOCKS):
                 nc.tensor.matmul(
                     bank[:],
-                    w_blocks[kb][:],
+                    weights[:, kb, :],
                     table_blocks[kb][:].indirect(piece_offsets),
                     start=(kb == 0),
                     stop=(kb == K_BLOCKS - 1),
                 )
             staged = staging.tile([P, PIECE], F32, name="staged")
-            nc.vector.tensor_scalar(staged[:], bank[:], bias[:, 0:1], None, mybir.AluOpType.add)
-            nc.sync.dma_start(out[:, piece * PIECE : (piece + 1) * PIECE], staged[:])
+            piece_out = out[:, piece * PIECE : (piece + 1) * PIECE]
+            if piece % 2 == 0:
+                nc.vector.tensor_scalar(staged[:], bank[:], bias[:, 0:1], None, mybir.AluOpType.add)
+                nc.sync.dma_start(piece_out, staged[:])
+            else:
+                nc.scalar.activation(
+                    staged[:], bank[:], mybir.ActivationFunctionType.Identity, bias=bias[:, 0:1]
+                )
+                nc.scalar.dma_start(piece_out, staged[:])

@@ -18,21 +18,22 @@ def tile_gather_matmul_kernel(tc, table, w, b, offs, out):
     with (
         tc.tile_pool(name="held", bufs=1) as held,
         tc.tile_pool(name="staging", bufs=PIECES) as staging,
-        tc.psum_pool(name="psum", bufs=PIECES) as psum,
+        tc.psum_pool(name="psum", bufs=3) as psum,
         tc.psum_pool(name="idle", bufs=1) as idle,
     ):
         offsets = held.tile([P, N // 16], U16, name="offsets")
         nc.sync.dma_start(offsets[:], offs)
 
+        bias = held.tile([P, 1], F32, name="bias")
+        nc.scalar.dma_start(bias[:], b)
         weights = held.tile([P, K_BLOCKS, M], BF16, name="weights")
         nc.scalar.dma_start(weights[:], w.rearrange("(kb p) m -> p kb m", p=P))
 
         table_blocks = [held.tile([P, S], BF16, name=f"table{kb}") for kb in range(K_BLOCKS)]
-        nc.sync.dma_start(table_blocks[0][:], table[0:P, :])
-        nc.scalar.dma_start(table_blocks[1][:], table[P : 2 * P, :])
-
-        bias = held.tile([P, 1], F32, name="bias")
-        nc.sync.dma_start(bias[:], b)
+        for kb in range(K_BLOCKS):
+            rows = slice(kb * P, (kb + 1) * P)
+            nc.sync.dma_start(table_blocks[kb][:, : S // 2], table[rows, : S // 2])
+            nc.scalar.dma_start(table_blocks[kb][:, S // 2 :], table[rows, S // 2 :])
 
         zeros = held.tile([P, 128], BF16, name="zeros")
         nc.vector.memset(zeros[:], 0.0)

@@ -5,10 +5,11 @@ BF16, F32, U16 = mybir.dt.bfloat16, mybir.dt.float32, mybir.dt.uint16
 P = 128
 K, S, M, N = 256, 1024, 128, 1536
 K_BLOCKS = K // P
-PIECE = 256
+PIECE = 512
 PIECES = N // PIECE
 PIECE_COLS = PIECE // 16
-WARM_UP = 16
+
+WARM_UP = 12
 
 FLOPS = 2 * K * M * N
 
@@ -18,28 +19,26 @@ def tile_gather_matmul_kernel(tc, table, w, b, offs, out):
     with (
         tc.tile_pool(name="held", bufs=1) as held,
         tc.tile_pool(name="staging", bufs=PIECES) as staging,
-        tc.psum_pool(name="psum", bufs=3) as psum,
+        tc.psum_pool(name="psum", bufs=PIECES) as psum,
         tc.psum_pool(name="idle", bufs=1) as idle,
     ):
         offsets = held.tile([P, N // 16], U16, name="offsets")
         nc.sync.dma_start(offsets[:], offs)
 
-        bias = held.tile([P, 1], F32, name="bias")
-        nc.scalar.dma_start(bias[:], b)
-        weights = held.tile([P, K_BLOCKS, M], BF16, name="weights")
-        nc.scalar.dma_start(weights[:], w.rearrange("(kb p) m -> p kb m", p=P))
-
         table_blocks = [held.tile([P, S], BF16, name=f"table{kb}") for kb in range(K_BLOCKS)]
+        w_blocks = [held.tile([P, M], BF16, name=f"w{kb}") for kb in range(K_BLOCKS)]
         for kb in range(K_BLOCKS):
             rows = slice(kb * P, (kb + 1) * P)
-            nc.sync.dma_start(table_blocks[kb][:, : S // 2], table[rows, : S // 2])
-            nc.scalar.dma_start(table_blocks[kb][:, S // 2 :], table[rows, S // 2 :])
+            nc.sync.dma_start(w_blocks[kb][:], w[rows, :])
+            nc.sync.dma_start(table_blocks[kb][:], table[rows, :])
+        bias = held.tile([P, 1], F32, name="bias")
+        nc.sync.dma_start(bias[:], b)
 
-        zeros = held.tile([P, 128], BF16, name="zeros")
+        zeros = held.tile([P, M], BF16, name="zeros")
         nc.vector.memset(zeros[:], 0.0)
-        unread = idle.tile([P, 128], F32, name="unread")
+        unread = idle.tile([P, M], F32, name="unread")
         for i in range(WARM_UP):
-            nc.tensor.matmul(unread[:], zeros[:, :M], zeros[:], start=True, stop=True)
+            nc.tensor.matmul(unread[:], zeros[:], zeros[:], start=True, stop=True)
 
         for piece in range(PIECES):
             piece_offsets = offsets[:, piece * PIECE_COLS : (piece + 1) * PIECE_COLS]
@@ -47,18 +46,11 @@ def tile_gather_matmul_kernel(tc, table, w, b, offs, out):
             for kb in range(K_BLOCKS):
                 nc.tensor.matmul(
                     bank[:],
-                    weights[:, kb, :],
+                    w_blocks[kb][:],
                     table_blocks[kb][:].indirect(piece_offsets),
                     start=(kb == 0),
                     stop=(kb == K_BLOCKS - 1),
                 )
             staged = staging.tile([P, PIECE], F32, name="staged")
-            piece_out = out[:, piece * PIECE : (piece + 1) * PIECE]
-            if piece % 2 == 0:
-                nc.vector.tensor_scalar(staged[:], bank[:], bias[:, 0:1], None, mybir.AluOpType.add)
-                nc.sync.dma_start(piece_out, staged[:])
-            else:
-                nc.scalar.activation(
-                    staged[:], bank[:], mybir.ActivationFunctionType.Identity, bias=bias[:, 0:1]
-                )
-                nc.scalar.dma_start(piece_out, staged[:])
+            nc.vector.tensor_scalar(staged[:], bank[:], bias[:, 0:1], None, mybir.AluOpType.add)
+            nc.sync.dma_start(out[:, piece * PIECE : (piece + 1) * PIECE], staged[:])

@@ -5,9 +5,19 @@ BF16, F32, U16 = mybir.dt.bfloat16, mybir.dt.float32, mybir.dt.uint16
 P = 128
 K, S, M, N = 256, 1024, 128, 1536
 K_BLOCKS = K // P
-PIECE = 512
-PIECES = N // PIECE
-PIECE_COLS = PIECE // 16
+BANK = 512
+SMALLEST = 128
+EARLY = 2
+
+
+def cut_list():
+    widths = [BANK] * (N // BANK - 1)
+    rest = BANK
+    while rest > SMALLEST:
+        rest //= 2
+        widths.append(rest)
+    widths.append(rest)
+    return widths
 
 WARM_UP = 12
 
@@ -16,10 +26,12 @@ FLOPS = 2 * K * M * N
 
 def tile_gather_matmul_kernel(tc, table, w, b, offs, out):
     nc = tc.nc
+    widths = cut_list()
+    pieces = len(widths)
     with (
         tc.tile_pool(name="held", bufs=1) as held,
-        tc.tile_pool(name="staging", bufs=PIECES) as staging,
-        tc.psum_pool(name="psum", bufs=PIECES) as psum,
+        tc.tile_pool(name="staging", bufs=pieces) as staging,
+        tc.psum_pool(name="psum", bufs=pieces) as psum,
         tc.psum_pool(name="idle", bufs=1) as idle,
     ):
         offsets = held.tile([P, N // 16], U16, name="offsets")
@@ -40,17 +52,20 @@ def tile_gather_matmul_kernel(tc, table, w, b, offs, out):
         for i in range(WARM_UP):
             nc.tensor.matmul(unread[:], zeros[:], zeros[:], start=True, stop=True)
 
-        for piece in range(PIECES):
-            piece_offsets = offsets[:, piece * PIECE_COLS : (piece + 1) * PIECE_COLS]
-            bank = psum.tile([P, PIECE], F32, name="bank")
-            for kb in range(K_BLOCKS):
+        first = 0
+        for piece, width in enumerate(widths):
+            piece_offsets = offsets[:, first // 16 : (first + width) // 16]
+            bank = psum.tile([P, width], F32, name="bank")
+            blocks = list(range(K_BLOCKS)) if piece < EARLY else list(reversed(range(K_BLOCKS)))
+            for turn, kb in enumerate(blocks):
                 nc.tensor.matmul(
                     bank[:],
                     w_blocks[kb][:],
                     table_blocks[kb][:].indirect(piece_offsets),
-                    start=(kb == 0),
-                    stop=(kb == K_BLOCKS - 1),
+                    start=(turn == 0),
+                    stop=(turn == K_BLOCKS - 1),
                 )
-            staged = staging.tile([P, PIECE], F32, name="staged")
+            staged = staging.tile([P, width], F32, name="staged")
             nc.vector.tensor_scalar(staged[:], bank[:], bias[:, 0:1], None, mybir.AluOpType.add)
-            nc.sync.dma_start(out[:, piece * PIECE : (piece + 1) * PIECE], staged[:])
+            nc.sync.dma_start(out[:, first : first + width], staged[:])
+            first += width

@@ -19,8 +19,6 @@ def cut_list():
     widths.append(rest)
     return widths
 
-WARM_UP = 12
-
 FLOPS = 2 * K * M * N
 
 
@@ -32,7 +30,6 @@ def tile_gather_matmul_kernel(tc, table, w, b, offs, out):
         tc.tile_pool(name="held", bufs=1) as held,
         tc.tile_pool(name="staging", bufs=pieces) as staging,
         tc.psum_pool(name="psum", bufs=pieces) as psum,
-        tc.psum_pool(name="idle", bufs=1) as idle,
     ):
         offsets = held.tile([P, N // 16], U16, name="offsets")
         nc.sync.dma_start(offsets[:], offs)
@@ -45,12 +42,6 @@ def tile_gather_matmul_kernel(tc, table, w, b, offs, out):
             nc.sync.dma_start(table_blocks[kb][:], table[rows, :])
         bias = held.tile([P, 1], F32, name="bias")
         nc.sync.dma_start(bias[:], b)
-
-        zeros = held.tile([P, M], BF16, name="zeros")
-        nc.vector.memset(zeros[:], 0.0)
-        unread = idle.tile([P, M], F32, name="unread")
-        for i in range(WARM_UP):
-            nc.tensor.matmul(unread[:], zeros[:], zeros[:], start=True, stop=True)
 
         first = 0
         for piece, width in enumerate(widths):

@@ -5,19 +5,15 @@ BF16, F32, U16 = mybir.dt.bfloat16, mybir.dt.float32, mybir.dt.uint16
 P = 128
 K, S, M, N = 256, 1024, 128, 1536
 K_BLOCKS = K // P
-BANK = 512
-SMALLEST = 128
+STEP = 128
 EARLY = 2
 
 
 def cut_list():
-    widths = [BANK] * (N // BANK - 1)
-    rest = BANK
-    while rest > SMALLEST:
-        rest //= 2
-        widths.append(rest)
-    widths.append(rest)
+    widths = [steps * STEP for steps in (3, 2, 1) for twice in range(2)]
+    assert sum(widths) == N
     return widths
+
 
 FLOPS = 2 * K * M * N
 

@@ -5,12 +5,12 @@ BF16, F32, U16 = mybir.dt.bfloat16, mybir.dt.float32, mybir.dt.uint16
 P = 128
 K, S, M, N = 256, 1024, 128, 1536
 K_BLOCKS = K // P
-STEP = 128
-EARLY = 2
+PIECE = 256
+EARLY = 3
 
 
 def cut_list():
-    widths = [steps * STEP for steps in (3, 2, 1) for twice in range(2)]
+    widths = [PIECE] * (N // PIECE - 1) + [PIECE // 2] * 2
     assert sum(widths) == N
     return widths
 

@@ -35,7 +35,7 @@ def tile_gather_matmul_kernel(tc, table, w, b, offs, out):
         for kb in range(K_BLOCKS):
             rows = slice(kb * P, (kb + 1) * P)
             nc.sync.dma_start(w_blocks[kb][:], w[rows, :])
-            nc.sync.dma_start(table_blocks[kb][:], table[rows, :])
+            nc.scalar.dma_start(table_blocks[kb][:], table[rows, :])
         bias = held.tile([P, 1], F32, name="bias")
         nc.sync.dma_start(bias[:], b)
 

import concourse.mybir as mybir

BF16, F32, U16 = mybir.dt.bfloat16, mybir.dt.float32, mybir.dt.uint16

P = 128
K, S, M, N = 256, 1024, 128, 1536
K_BLOCKS = K // P
PIECE = 256
EARLY = 3


def cut_list():
    widths = [PIECE] * (N // PIECE - 1) + [PIECE // 2] * 2
    assert sum(widths) == N
    return widths


FLOPS = 2 * K * M * N


def tile_gather_matmul_kernel(tc, table, w, b, offs, out):
    nc = tc.nc
    widths = cut_list()
    pieces = len(widths)
    with (
        tc.tile_pool(name="held", bufs=1) as held,
        tc.tile_pool(name="staging", bufs=pieces) as staging,
        tc.psum_pool(name="psum", bufs=pieces) as psum,
    ):
        offsets = held.tile([P, N // 16], U16, name="offsets")
        nc.sync.dma_start(offsets[:], offs)

        table_blocks = [held.tile([P, S], BF16, name=f"table{kb}") for kb in range(K_BLOCKS)]
        w_blocks = [held.tile([P, M], BF16, name=f"w{kb}") for kb in range(K_BLOCKS)]
        for kb in range(K_BLOCKS):
            rows = slice(kb * P, (kb + 1) * P)
            nc.sync.dma_start(w_blocks[kb][:], w[rows, :])
            nc.scalar.dma_start(table_blocks[kb][:], table[rows, :])
        bias = held.tile([P, 1], F32, name="bias")
        nc.sync.dma_start(bias[:], b)

        first = 0
        for piece, width in enumerate(widths):
            piece_offsets = offsets[:, first // 16 : (first + width) // 16]
            bank = psum.tile([P, width], F32, name="bank")
            blocks = list(range(K_BLOCKS)) if piece < EARLY else list(reversed(range(K_BLOCKS)))
            for turn, kb in enumerate(blocks):
                nc.tensor.matmul(
                    bank[:],
                    w_blocks[kb][:],
                    table_blocks[kb][:].indirect(piece_offsets),
                    start=(turn == 0),
                    stop=(turn == K_BLOCKS - 1),
                )
            staged = staging.tile([P, width], F32, name="staged")
            nc.vector.tensor_scalar(staged[:], bank[:], bias[:, 0:1], None, mybir.AluOpType.add)
            nc.sync.dma_start(out[:, first : first + width], staged[:])
            first += width
